import numpy as np
import ml_dtypes


def mxq(x, axis, fmt="e4m3"):
    dtype, down = {"e4m3": (ml_dtypes.float8_e4m3fn, 7), "e5m2": (ml_dtypes.float8_e5m2, 14)}[fmt]
    v = np.moveaxis(np.asarray(x, np.float32).astype(ml_dtypes.bfloat16).astype(np.float64), axis, -1)
    blocks = v.reshape(v.shape[:-1] + (-1, 32))
    amax = np.abs(blocks).max(-1, keepdims=True)
    byte = np.maximum(np.where(amax > 0, np.frexp(amax)[1] - 1 + 127, 0) - down, 1)
    scale = np.exp2(byte - 127.0)
    codes = (blocks / scale).astype(np.float32).astype(dtype).astype(np.float64)
    return np.moveaxis((codes * scale).reshape(v.shape), -1, axis)


WIDE = False


def mx_kscale(k):
    if not WIDE:
        return np.ones(k)
    levels = np.array([30, -30])
    if k % 512:
        return np.exp2(np.random.permutation(np.resize(levels, k // 32))).repeat(32)
    a = np.empty((k // 512, 16))
    for p in range(k // 512):
        a[p, :8] = np.random.permutation(np.resize(levels, 8))
        for g in range(8):
            far = levels[np.abs(levels - a[p, g]) >= 10]
            a[p, g + 8] = far[np.random.randint(len(far))]
    return np.exp2(a.ravel()).repeat(32)


def f64(x):
    return np.asarray(x).astype(np.float64)


def striped(idx):
    return np.tile(np.asarray(idx).reshape(-1, 16).T, (8, 1)).astype(np.uint16)


def unstriped(offs):
    return offs[:16].T.reshape(-1).astype(np.int64)


E2M1 = np.array([0.0, 0.5, 1.0, 1.5, 2.0, 3.0, 4.0, 6.0, -0.0, -0.5, -1.0, -1.5, -2.0, -3.0, -4.0, -6.0])


def pack_weight(w, fmt):
    k, n = w.shape
    w = f64(np.asarray(w, np.float32).astype(ml_dtypes.bfloat16)).reshape(k // 32, 32, n)
    amax = np.abs(w).max(1)
    if fmt in ("e4m3", "e5m2"):
        byte = np.frexp(amax)[1] - 1 + 127 - (7 if fmt == "e4m3" else 14)
    else:
        mant, ex = np.frexp(amax / 6.0)
        byte = np.where(mant > 0.5, ex, ex - 1) + 127
    byte = np.clip(np.where(amax > 0, byte, 1), 1, 254)
    scaled = (w * np.exp2(127.0 - byte)[:, None, :]).reshape(k, n).astype(np.float32)
    by_word = np.ascontiguousarray(scaled.reshape(k // 512, 128, 4, n).transpose(0, 1, 3, 2))
    if fmt in ("e4m3", "e5m2"):
        words = by_word.astype(ml_dtypes.float8_e4m3fn if fmt == "e4m3" else ml_dtypes.float8_e5m2).view(np.uint8)
    else:
        c = by_word.astype(ml_dtypes.float4_e2m1fn).view(np.uint8) & 0xF
        words = (c[..., 0::2] | (c[..., 1::2] << 4)).reshape(k // 512, 128, 2 * n)
    return np.ascontiguousarray(words), np.ascontiguousarray(byte.astype(np.uint8).reshape(k // 512, 16, n))


def unpack_weight(words, scales, fmt):
    g, _, n = scales.shape
    words = np.ascontiguousarray(words).reshape(g, 128, n, -1)
    if fmt in ("e4m3", "e5m2"):
        vals = words.view(ml_dtypes.float8_e4m3fn if fmt == "e4m3" else ml_dtypes.float8_e5m2).astype(np.float64)
    else:
        nib = np.empty((g, 128, n, 4), np.uint8)
        nib[..., 0::2] = words & 0xF
        nib[..., 1::2] = words >> 4
        vals = E2M1[nib]
    vals = vals * np.repeat(np.exp2(scales.astype(np.float64) - 127.0), 8, axis=1)[..., None]
    return vals.transpose(0, 1, 3, 2).reshape(g * 512, n)


K, T, J, I, M = 1024, 1024, 256, 256, 128


def setup_inputs():
    n = np.random.standard_normal
    idx = np.random.permutation(T)[:J]
    idx2 = np.random.permutation(I)[:M]
    fk = mx_kscale(K)
    xtp = pack_weight(n((K, T)) * 0.04 * fk[:, None], "e5m2")
    return {
        "xt_words": xtp[0],
        "xt_scales": xtp[1],
        "ky": (n((K, I)) / fk[:, None]).astype(np.float32),
        "bi": (np.random.uniform(-0.7, 0.7, (1, I))).astype(np.float32),
        "rs": (1.0 * n((J, M))).astype(np.float32),
        "offs": striped(idx),
        "offs2": striped(idx2),
    }


def reference(xt_words, xt_scales, ky, bi, rs, offs, offs2):
    idx = unstriped(offs)
    idx2 = unstriped(offs2)
    xtu = unpack_weight(xt_words, xt_scales, "e5m2")
    xtidxg = xtu[:, idx]
    kyq = mxq(f64(ky), 0, "e4m3")
    a0 = xtidxg.T @ kyq
    a = a0 + f64(bi)
    mn = np.mean(np.abs(a), axis=1, keepdims=True)
    y = a[:, idx2] / mn + 0.5 * f64(rs)
    return y

@@ -1,0 +1,144 @@
+from contextlib import ExitStack
+
+import concourse.mybir as mybir
+from concourse.masks import make_identity
+
+K, T, J, I, M = 1024, 1024, 256, 256, 128
+FLOPS = 2 * K * J * I
+
+F32 = mybir.dt.float32
+BF16 = mybir.dt.bfloat16
+I32 = mybir.dt.int32
+U32 = mybir.dt.uint32
+U16 = mybir.dt.uint16
+U8 = mybir.dt.uint8
+E4M3X4 = mybir.dt.float8_e4m3fn_x4
+E5M2X4 = mybir.dt.float8_e5m2_x4
+ALU = mybir.AluOpType
+ACT = mybir.ActivationFunctionType
+
+P = 128
+PACK = 4
+PASSES = K // (P * PACK)
+ROW_TILES = J // P
+SCALAR_COLS = (256, 96)
+
+
+def tile_list_scores_picked_given_looked_kernel(tc, xt_words, xt_scales, ky, bi, rs, offs, offs2, out):
+    nc = tc.nc
+    with ExitStack() as ctx:
+        sb = ctx.enter_context(tc.tile_pool(name="sb", bufs=1))
+        ps = ctx.enter_context(tc.psum_pool(name="ps", bufs=1))
+
+        tokens = sb.tile([P, J // 16], U16, name="tokens")
+        places = sb.tile([P, M // 16], U16, name="places")
+        table_scales = sb.tile([P, PASSES * T], U8, name="table_scales", align_bytes=64)
+        table_words = [sb.tile([P, T], I32, name=f"table_words{z}", align_bytes=64) for z in range(PASSES)]
+        keys = [sb.tile([P, PACK, I], F32, name=f"keys{z}", align_bytes=64) for z in range(PASSES)]
+        bias_pairs = sb.tile([P, 2], F32, name="bias_pairs")
+        residual = sb.tile([P, ROW_TILES, M], F32, name="residual")
+        identity = sb.tile([P, P], F32, name="identity")
+
+        nc.vector.memset(table_scales[:].bitcast(I32), 0)
+        make_identity(nc, identity[:])
+
+        def load_keys(z):
+            rows = ky[z * P * PACK : (z + 1) * P * PACK, :]
+            nc.sync.dma_start(out=keys[z][:], in_=rows.rearrange("(p t) i -> p t i", t=PACK))
+
+        def load_words(z):
+            nc.sync.dma_start(out=table_words[z][:], in_=xt_words[z].rearrange("p c r -> p (c r)").bitcast(I32))
+
+        nc.scalar.dma_start(out=bias_pairs[:], in_=bi.rearrange("o (p e) -> (o p) e", e=2))
+        load_keys(0)
+        nc.sync.dma_start(tokens[:], offs)
+        scale_rows = table_scales[:].bitcast(I32).rearrange("p (z c) -> p z c", z=PASSES)
+        for q in range(4):
+            nc.sync.dma_start(
+                out=scale_rows[32 * q : 32 * q + 4],
+                in_=xt_scales[:, 4 * q : 4 * q + 4, :].bitcast(I32).rearrange("z r c -> r z c"),
+            )
+        load_keys(1)
+        load_words(0)
+        load_words(1)
+        nc.sync.dma_start(out=residual[:], in_=rs.rearrange("(h p) m -> p h m", p=P))
+        nc.sync.dma_start(places[:], offs2)
+
+        rounded = [sb.tile([P, I, PACK], BF16, name=f"rounded{z}", align_bytes=64) for z in range(PASSES)]
+        key_words = [sb.tile([P, I], U32, name=f"key_words{z}", align_bytes=64) for z in range(PASSES)]
+        key_scales = [sb.tile([P, I], U8, name=f"key_scales{z}", align_bytes=64) for z in range(PASSES)]
+        picked_scales = [sb.tile([P, J], U8, name=f"picked_scales{z}", align_bytes=64) for z in range(PASSES)]
+
+        def round_keys(z):
+            dst = rounded[z][:].rearrange("p (c i) t -> p c t i", i=4)
+            src = keys[z][:].rearrange("p t (c i) -> p c t i", i=4)
+            split = SCALAR_COLS[z] // 4
+            nc.scalar.copy(out=dst[:, :split], in_=src[:, :split])
+            if split < I // 4:
+                nc.vector.tensor_copy(out=dst[:, split:], in_=src[:, split:])
+
+        def quantise_keys(z):
+            nc.vector.quantize_mx(
+                out=key_words[z][:].bitcast(E4M3X4),
+                scales=key_scales[z][:],
+                in_=rounded[z][:].rearrange("p i t -> p (i t)"),
+            )
+
+        round_keys(0)
+        for z in range(PASSES):
+            nc.vector.tensor_copy(picked_scales[z][:], table_scales[:, z * T : (z + 1) * T].indirect(tokens[:]))
+        round_keys(1)
+        quantise_keys(0)
+        quantise_keys(1)
+
+        bias_bank = ps.tile([P, 2, P], F32, name="bias_bank")
+        for e in range(2):
+            nc.tensor.transpose(bias_bank[:, e, :], bias_pairs[:, e : e + 1].to_broadcast([P, P]), identity[:])
+        bias = sb.tile([P, I], F32, name="bias")
+        nc.scalar.copy(out=bias[:].rearrange("p (c e) -> p c e", e=2), in_=bias_bank[:].rearrange("p e c -> p c e"))
+
+        first_words = sb.tile([P, J], U32, name="first_words", align_bytes=64)
+        nc.vector.tensor_copy(first_words[:], table_words[0][:].bitcast(U32).indirect(tokens[:]))
+        acc = [ps.tile([P, I], F32, name=f"acc{h}") for h in range(ROW_TILES)]
+
+        def multiply(h, z, words):
+            nc.tensor.matmul_mx(
+                out=acc[h][:],
+                lhsT=words.bitcast(E5M2X4),
+                lhsT_scale=picked_scales[z][:, h * P : (h + 1) * P],
+                rhs=key_words[z][:].bitcast(E4M3X4),
+                rhs_scale=key_scales[z][:],
+                start=(z == 0),
+                stop=(z == PASSES - 1),
+            )
+
+        for h in range(ROW_TILES):
+            multiply(h, 0, first_words[:, h * P : (h + 1) * P])
+        for h in range(ROW_TILES):
+            last_words = sb.tile([P, P], U32, name=f"last_words{h}", align_bytes=64)
+            nc.vector.tensor_copy(
+                last_words[:], table_words[1][:].bitcast(U32).indirect(tokens[:, h * P // 16 : (h + 1) * P // 16])
+            )
+            multiply(h, 1, last_words[:])
+
+        half_residual = sb.tile([P, ROW_TILES, M], F32, name="half_residual")
+        nc.scalar.activation(out=half_residual[:], in_=residual[:], func=ACT.Copy, scale=0.5)
+
+        scores = [sb.tile([P, I], F32, name=f"scores{h}") for h in range(ROW_TILES)]
+        means = [sb.tile([P, 1], F32, name=f"means{h}") for h in range(ROW_TILES)]
+        picked = [sb.tile([P, M], F32, name=f"picked{h}") for h in range(ROW_TILES)]
+        for h in range(ROW_TILES):
+            nc.vector.tensor_tensor(out=scores[h][:], in0=acc[h][:], in1=bias[:], op=ALU.add)
+            magnitudes = sb.tile([P, I], F32, name=f"magnitudes{h}")
+            nc.scalar.activation(
+                out=magnitudes[:], in_=scores[h][:], func=ACT.Abs, scale=1.0 / I, accum_out=means[h][:]
+            )
+        for h in range(ROW_TILES):
+            nc.vector.tensor_copy(picked[h][:], scores[h][:].indirect(places[:]))
+            inverse = sb.tile([P, 1], F32, name=f"inverse{h}")
+            nc.vector.reciprocal(out=inverse[:], in_=means[h][:])
+            result = sb.tile([P, M], F32, name=f"result{h}")
+            nc.vector.scalar_tensor_tensor(
+                out=result[:], in0=picked[h][:], scalar=inverse[:], in1=half_residual[:, h, :], op0=ALU.mult, op1=ALU.add
+            )
+            nc.sync.dma_start(out=out[h * P : (h + 1) * P, :], in_=result[:])

@@ -21,7 +21,7 @@ P = 128
 PACK = 4
 PASSES = K // (P * PACK)
 ROW_TILES = J // P
-SCALAR_COLS = (256, 96)
+SCALAR_COLS = (256, 256)
 
 
 def tile_list_scores_picked_given_looked_kernel(tc, xt_words, xt_scales, ky, bi, rs, offs, offs2, out):
@@ -39,7 +39,8 @@ def tile_list_scores_picked_given_looked_kernel(tc, xt_words, xt_scales, ky, bi,
         residual = sb.tile([P, ROW_TILES, M], F32, name="residual")
         identity = sb.tile([P, P], F32, name="identity")
 
-        nc.vector.memset(table_scales[:].bitcast(I32), 0)
+        nc.gpsimd.memset(table_scales[:].bitcast(I32), 0)
+        nc.gpsimd.dma_start(out=bias_pairs[:], in_=bi.rearrange("o (p e) -> (o p) e", e=2))
         make_identity(nc, identity[:])
 
         def load_keys(z):
@@ -49,14 +50,13 @@ def tile_list_scores_picked_given_looked_kernel(tc, xt_words, xt_scales, ky, bi,
         def load_words(z):
             nc.sync.dma_start(out=table_words[z][:], in_=xt_words[z].rearrange("p c r -> p (c r)").bitcast(I32))
 
-        nc.scalar.dma_start(out=bias_pairs[:], in_=bi.rearrange("o (p e) -> (o p) e", e=2))
-        load_keys(0)
         nc.sync.dma_start(tokens[:], offs)
+        load_keys(0)
         scale_rows = table_scales[:].bitcast(I32).rearrange("p (z c) -> p z c", z=PASSES)
-        for q in range(4):
+        for r in range(4):
             nc.sync.dma_start(
-                out=scale_rows[32 * q : 32 * q + 4],
-                in_=xt_scales[:, 4 * q : 4 * q + 4, :].bitcast(I32).rearrange("z r c -> r z c"),
+                out=scale_rows[r:P:32],
+                in_=xt_scales[:, r:16:4, :].bitcast(I32).rearrange("z q c -> q z c"),
             )
         load_keys(1)
         load_words(0)
@@ -84,18 +84,18 @@ def tile_list_scores_picked_given_looked_kernel(tc, xt_words, xt_scales, ky, bi,
                 in_=rounded[z][:].rearrange("p i t -> p (i t)"),
             )
 
+        bias_bank = ps.tile([P, 2, P], F32, name="bias_bank")
+        for e in range(2):
+            nc.tensor.transpose(bias_bank[:, e, :], bias_pairs[:, e : e + 1].to_broadcast([P, P]), identity[:])
+        bias = sb.tile([P, I], F32, name="bias")
+        nc.scalar.copy(out=bias[:].rearrange("p (c e) -> p c e", e=2), in_=bias_bank[:].rearrange("p e c -> p c e"))
+
         round_keys(0)
         for z in range(PASSES):
             nc.vector.tensor_copy(picked_scales[z][:], table_scales[:, z * T : (z + 1) * T].indirect(tokens[:]))
         round_keys(1)
         quantise_keys(0)
         quantise_keys(1)
-
-        bias_bank = ps.tile([P, 2, P], F32, name="bias_bank")
-        for e in range(2):
-            nc.tensor.transpose(bias_bank[:, e, :], bias_pairs[:, e : e + 1].to_broadcast([P, P]), identity[:])
-        bias = sb.tile([P, I], F32, name="bias")
-        nc.scalar.copy(out=bias[:].rearrange("p (c e) -> p c e", e=2), in_=bias_bank[:].rearrange("p e c -> p c e"))
 
         first_words = sb.tile([P, J], U32, name="first_words", align_bytes=64)
         nc.vector.tensor_copy(first_words[:], table_words[0][:].bitcast(U32).indirect(tokens[:]))
@@ -133,12 +133,19 @@ def tile_list_scores_picked_given_looked_kernel(tc, xt_words, xt_scales, ky, bi,
             nc.scalar.activation(
                 out=magnitudes[:], in_=scores[h][:], func=ACT.Abs, scale=1.0 / I, accum_out=means[h][:]
             )
+        inverses = [sb.tile([P, 1], F32, name=f"inverses{h}") for h in range(ROW_TILES)]
         for h in range(ROW_TILES):
             nc.vector.tensor_copy(picked[h][:], scores[h][:].indirect(places[:]))
-            inverse = sb.tile([P, 1], F32, name=f"inverse{h}")
-            nc.vector.reciprocal(out=inverse[:], in_=means[h][:])
+        for h in range(ROW_TILES):
+            nc.vector.reciprocal(out=inverses[h][:], in_=means[h][:])
+        for h in range(ROW_TILES):
             result = sb.tile([P, M], F32, name=f"result{h}")
             nc.vector.scalar_tensor_tensor(
-                out=result[:], in0=picked[h][:], scalar=inverse[:], in1=half_residual[:, h, :], op0=ALU.mult, op1=ALU.add
+                out=result[:],
+                in0=picked[h][:],
+                scalar=inverses[h][:],
+                in1=half_residual[:, h, :],
+                op0=ALU.mult,
+                op1=ALU.add,
             )
             nc.sync.dma_start(out=out[h * P : (h + 1) * P, :], in_=result[:])

from contextlib import ExitStack

import concourse.mybir as mybir
from concourse.masks import make_identity

K, T, J, I, M = 1024, 1024, 256, 256, 128
FLOPS = 2 * K * J * I

F32 = mybir.dt.float32
BF16 = mybir.dt.bfloat16
I32 = mybir.dt.int32
U32 = mybir.dt.uint32
U16 = mybir.dt.uint16
U8 = mybir.dt.uint8
E4M3X4 = mybir.dt.float8_e4m3fn_x4
E5M2X4 = mybir.dt.float8_e5m2_x4
ALU = mybir.AluOpType
ACT = mybir.ActivationFunctionType

P = 128
PACK = 4
PASSES = K // (P * PACK)
ROW_TILES = J // P
SCALAR_COLS = (256, 256)


def tile_list_scores_picked_given_looked_kernel(tc, xt_words, xt_scales, ky, bi, rs, offs, offs2, out):
    nc = tc.nc
    with ExitStack() as ctx:
        sb = ctx.enter_context(tc.tile_pool(name="sb", bufs=1))
        ps = ctx.enter_context(tc.psum_pool(name="ps", bufs=1))

        tokens = sb.tile([P, J // 16], U16, name="tokens")
        places = sb.tile([P, M // 16], U16, name="places")
        table_scales = sb.tile([P, PASSES * T], U8, name="table_scales", align_bytes=64)
        table_words = [sb.tile([P, T], I32, name=f"table_words{z}", align_bytes=64) for z in range(PASSES)]
        keys = [sb.tile([P, PACK, I], F32, name=f"keys{z}", align_bytes=64) for z in range(PASSES)]
        bias_pairs = sb.tile([P, 2], F32, name="bias_pairs")
        residual = sb.tile([P, ROW_TILES, M], F32, name="residual")
        identity = sb.tile([P, P], F32, name="identity")

        nc.gpsimd.memset(table_scales[:].bitcast(I32), 0)
        nc.gpsimd.dma_start(out=bias_pairs[:], in_=bi.rearrange("o (p e) -> (o p) e", e=2))
        make_identity(nc, identity[:])

        def load_keys(z):
            rows = ky[z * P * PACK : (z + 1) * P * PACK, :]
            nc.sync.dma_start(out=keys[z][:], in_=rows.rearrange("(p t) i -> p t i", t=PACK))

        def load_words(z):
            nc.sync.dma_start(out=table_words[z][:], in_=xt_words[z].rearrange("p c r -> p (c r)").bitcast(I32))

        nc.sync.dma_start(tokens[:], offs)
        load_keys(0)
        scale_rows = table_scales[:].bitcast(I32).rearrange("p (z c) -> p z c", z=PASSES)
        for r in range(4):
            nc.sync.dma_start(
                out=scale_rows[r:P:32],
                in_=xt_scales[:, r:16:4, :].bitcast(I32).rearrange("z q c -> q z c"),
            )
        load_keys(1)
        load_words(0)
        load_words(1)
        nc.sync.dma_start(out=residual[:], in_=rs.rearrange("(h p) m -> p h m", p=P))
        nc.sync.dma_start(places[:], offs2)

        rounded = [sb.tile([P, I, PACK], BF16, name=f"rounded{z}", align_bytes=64) for z in range(PASSES)]
        key_words = [sb.tile([P, I], U32, name=f"key_words{z}", align_bytes=64) for z in range(PASSES)]
        key_scales = [sb.tile([P, I], U8, name=f"key_scales{z}", align_bytes=64) for z in range(PASSES)]
        picked_scales = [sb.tile([P, J], U8, name=f"picked_scales{z}", align_bytes=64) for z in range(PASSES)]

        def round_keys(z):
            dst = rounded[z][:].rearrange("p (c i) t -> p c t i", i=4)
            src = keys[z][:].rearrange("p t (c i) -> p c t i", i=4)
            split = SCALAR_COLS[z] // 4
            nc.scalar.copy(out=dst[:, :split], in_=src[:, :split])
            if split < I // 4:
                nc.vector.tensor_copy(out=dst[:, split:], in_=src[:, split:])

        def quantise_keys(z):
            nc.vector.quantize_mx(
                out=key_words[z][:].bitcast(E4M3X4),
                scales=key_scales[z][:],
                in_=rounded[z][:].rearrange("p i t -> p (i t)"),
            )

        bias_bank = ps.tile([P, 2, P], F32, name="bias_bank")
        for e in range(2):
            nc.tensor.transpose(bias_bank[:, e, :], bias_pairs[:, e : e + 1].to_broadcast([P, P]), identity[:])
        bias = sb.tile([P, I], F32, name="bias")
        nc.scalar.copy(out=bias[:].rearrange("p (c e) -> p c e", e=2), in_=bias_bank[:].rearrange("p e c -> p c e"))

        round_keys(0)
        for z in range(PASSES):
            nc.vector.tensor_copy(picked_scales[z][:], table_scales[:, z * T : (z + 1) * T].indirect(tokens[:]))
        round_keys(1)
        quantise_keys(0)
        quantise_keys(1)

        first_words = sb.tile([P, J], U32, name="first_words", align_bytes=64)
        nc.vector.tensor_copy(first_words[:], table_words[0][:].bitcast(U32).indirect(tokens[:]))
        acc = [ps.tile([P, I], F32, name=f"acc{h}") for h in range(ROW_TILES)]

        def multiply(h, z, words):
            nc.tensor.matmul_mx(
                out=acc[h][:],
                lhsT=words.bitcast(E5M2X4),
                lhsT_scale=picked_scales[z][:, h * P : (h + 1) * P],
                rhs=key_words[z][:].bitcast(E4M3X4),
                rhs_scale=key_scales[z][:],
                start=(z == 0),
                stop=(z == PASSES - 1),
            )

        for h in range(ROW_TILES):
            multiply(h, 0, first_words[:, h * P : (h + 1) * P])
        for h in range(ROW_TILES):
            last_words = sb.tile([P, P], U32, name=f"last_words{h}", align_bytes=64)
            nc.vector.tensor_copy(
                last_words[:], table_words[1][:].bitcast(U32).indirect(tokens[:, h * P // 16 : (h + 1) * P // 16])
            )
            multiply(h, 1, last_words[:])

        half_residual = sb.tile([P, ROW_TILES, M], F32, name="half_residual")
        nc.scalar.activation(out=half_residual[:], in_=residual[:], func=ACT.Copy, scale=0.5)

        scores = [sb.tile([P, I], F32, name=f"scores{h}") for h in range(ROW_TILES)]
        means = [sb.tile([P, 1], F32, name=f"means{h}") for h in range(ROW_TILES)]
        picked = [sb.tile([P, M], F32, name=f"picked{h}") for h in range(ROW_TILES)]
        for h in range(ROW_TILES):
            nc.vector.tensor_tensor(out=scores[h][:], in0=acc[h][:], in1=bias[:], op=ALU.add)
            magnitudes = sb.tile([P, I], F32, name=f"magnitudes{h}")
            nc.scalar.activation(
                out=magnitudes[:], in_=scores[h][:], func=ACT.Abs, scale=1.0 / I, accum_out=means[h][:]
            )
        inverses = [sb.tile([P, 1], F32, name=f"inverses{h}") for h in range(ROW_TILES)]
        for h in range(ROW_TILES):
            nc.vector.tensor_copy(picked[h][:], scores[h][:].indirect(places[:]))
        for h in range(ROW_TILES):
            nc.vector.reciprocal(out=inverses[h][:], in_=means[h][:])
        for h in range(ROW_TILES):
            result = sb.tile([P, M], F32, name=f"result{h}")
            nc.vector.scalar_tensor_tensor(
                out=result[:],
                in0=picked[h][:],
                scalar=inverses[h][:],
                in1=half_residual[:, h, :],
                op0=ALU.mult,
                op1=ALU.add,
            )
            nc.sync.dma_start(out=out[h * P : (h + 1) * P, :], in_=result[:])
